import numpy as np
import ml_dtypes


def mxq(x, axis, fmt="e4m3"):
    dtype, down = {"e4m3": (ml_dtypes.float8_e4m3fn, 7), "e5m2": (ml_dtypes.float8_e5m2, 14)}[fmt]
    v = np.moveaxis(np.asarray(x, np.float32).astype(ml_dtypes.bfloat16).astype(np.float64), axis, -1)
    blocks = v.reshape(v.shape[:-1] + (-1, 32))
    amax = np.abs(blocks).max(-1, keepdims=True)
    byte = np.maximum(np.where(amax > 0, np.frexp(amax)[1] - 1 + 127, 0) - down, 1)
    scale = np.exp2(byte - 127.0)
    codes = (blocks / scale).astype(np.float32).astype(dtype).astype(np.float64)
    return np.moveaxis((codes * scale).reshape(v.shape), -1, axis)


WIDE = False


def mx_kscale(k):
    if not WIDE:
        return np.ones(k)
    levels = np.array([10, -10, 5, -5, 0])
    if k % 512:
        return np.exp2(np.random.permutation(np.resize(levels, k // 32))).repeat(32)
    a = np.empty((k // 512, 16))
    for p in range(k // 512):
        a[p, :8] = np.random.permutation(np.resize(levels, 8))
        for g in range(8):
            far = levels[np.abs(levels - a[p, g]) >= 10]
            a[p, g + 8] = far[np.random.randint(len(far))]
    return np.exp2(a.ravel()).repeat(32)


def f64(x):
    return np.asarray(x).astype(np.float64)


def striped(idx):
    return np.tile(idx.reshape(-1, 16).T, (8, 1)).astype(np.uint16)


def unstriped(offs):
    return offs[:16].T.reshape(-1).astype(np.int64)


def striped8(idx):
    return np.concatenate([x.reshape(-1, 16).T for x in idx]).astype(np.uint16)


def runs(offs, k):
    lists = np.stack([offs[16 * r : 16 * r + 16].T.reshape(-1) for r in range(8)]).astype(np.int64)
    return lists[np.arange(k) % 512 // 64]


def pack_weight(w):
    k, n = w.shape
    w = f64(np.asarray(w, np.float32).astype(ml_dtypes.bfloat16)).reshape(k // 32, 32, n)
    amax = np.abs(w).max(1)
    byte = np.clip(np.where(amax > 0, np.frexp(amax)[1] - 1 + 127 - 7, 1), 1, 254)
    scaled = (w * np.exp2(127.0 - byte)[:, None, :]).reshape(k, n).astype(np.float32)
    words = np.ascontiguousarray(scaled.reshape(k // 512, 128, 4, n).transpose(0, 1, 3, 2)).astype(ml_dtypes.float8_e4m3fn).view(np.uint8)
    return words, np.ascontiguousarray(byte.astype(np.uint8).reshape(k // 512, 16, n))


def unpack_weight(words, scales):
    g, p, n, _ = words.shape
    vals = np.ascontiguousarray(words).view(ml_dtypes.float8_e4m3fn).astype(np.float64) * np.repeat(np.exp2(scales.astype(np.float64) - 127.0), 8, axis=1)[..., None]
    return vals.transpose(0, 1, 3, 2).reshape(g * 512, n)


K, T, S, G, H, C, W = 512, 1024, 256, 2048, 512, 512, 192


def setup_inputs():
    n = np.random.standard_normal
    s = mx_kscale(K)[:, None]
    packed_xT = pack_weight(n((K, T)) * s)
    packed_dT = pack_weight(n((K, G)) / s)
    return {
        "x_words": packed_xT[0],
        "x_scales": packed_xT[1],
        "d_words": packed_dT[0],
        "d_scales": packed_dT[1],
        "gs": (np.random.uniform(0.5, 1.5, (K, 1)) / s).astype(np.float32),
        "offs": striped(np.random.permutation(T)[:S]),
        "k1": striped8(np.random.randint(0, G, (8, H))),
        "n1": striped8(np.stack([np.random.permutation(S) for _ in range(8)])),
        "n2": striped8(np.stack([np.random.permutation(S) for _ in range(8)])),
        "n3": striped8(np.stack([np.random.permutation(S) for _ in range(8)])),
        "cand": striped8(np.random.randint(0, T, (8, C))),
        "n4": striped(np.random.permutation(S)[:W]),
        "n5": striped(np.random.permutation(S)[:W]),
    }


def reference(x_words, x_scales, d_words, d_scales, gs, offs, k1, n1, n2, n3, cand, n4, n5):
    x_cand = unpack_weight(x_words, x_scales)[np.arange(K)[:, None], runs(cand, K)]
    d_k1 = unpack_weight(d_words, d_scales)[np.arange(K)[:, None], runs(k1, K)]
    xq = unpack_weight(x_words, x_scales)[:, unstriped(offs)]
    h = 0.0625 * (d_k1.T @ xq)
    st = h[np.arange(H)[:, None], runs(n1, H)] - (h[np.arange(H)[:, None], runs(n2, H)])
    z = f64(gs) * (np.maximum(st, st[np.arange(H)[:, None], runs(n3, H)]))
    s = 0.0625 * ((x_cand.T @ mxq(z, 0, "e4m3")))
    old = s[:, unstriped(n4)]
    pa = s[:, unstriped(n5)]
    ra = old - (0.5 * pa)
    out = s.copy()
    out[:, unstriped(n4)] = ra
    return out

@@ -1,0 +1,184 @@
+from contextlib import ExitStack
+
+import concourse.mybir as mybir
+
+K, T, S, G, H, C, W = 512, 1024, 256, 2048, 512, 512, 192
+FLOPS = 2 * K * H * S + 2 * K * C * S
+
+F32 = mybir.dt.float32
+BF16 = mybir.dt.bfloat16
+I32 = mybir.dt.int32
+U32 = mybir.dt.uint32
+U16 = mybir.dt.uint16
+U8 = mybir.dt.uint8
+FP8X4 = mybir.dt.float8_e4m3fn_x4
+ALU = mybir.AluOpType
+COPY = mybir.ActivationFunctionType.Copy
+
+P = 128
+PACK = 4
+HALF = S // 2
+SIXTEENTH = 0.0625
+
+
+def tile_picked_pqhcgapmxkdif_none_p_kernel(tc, x_words, x_scales, d_words, d_scales, gs, offs, k1, n1, n2, n3, cand, n4, n5, out):
+    nc = tc.nc
+    with ExitStack() as ctx:
+        lists = ctx.enter_context(tc.tile_pool(name="lists", bufs=1))
+        sb = ctx.enter_context(tc.tile_pool(name="sb", bufs=1))
+        ps = ctx.enter_context(tc.psum_pool(name="ps", bufs=1))
+
+        def load_list(name, src):
+            t = lists.tile(list(src.shape), U16, name=name)
+            nc.sync.dma_start(t[:], src)
+            return t
+
+        def load_scales(name, src, width):
+            t = sb.tile([P, width], U8, name=name, align_bytes=64)
+            rows = src[0].bitcast(I32)
+            nc.sync.dma_start(t[:].bitcast(I32), rows.unsqueeze(1).broadcast_to([16, 8, width // 4]))
+            return t
+
+        def load_words(name, src, width):
+            t = sb.tile([P, width], U32, name=name, align_bytes=64)
+            nc.sync.dma_start(t[:].bitcast(I32), src[0].rearrange("p n r -> p (n r)").bitcast(I32))
+            return t
+
+        def gather_packed(name, table, offsets, count, dtype):
+            t = sb.tile([P, count], dtype, name=name, align_bytes=64)
+            nc.vector.tensor_copy(t[:], table[:].indirect(offsets[:]))
+            return t
+
+        def place_odd_rows(dst, src):
+            for row in (1, 2, 3):
+                nc.scalar.dma_start(dst[row:P:32, :].bitcast(I32), src[8 * row : P : 32, :].bitcast(I32))
+
+        k1_t = load_list("k1_t", k1)
+        ds_table = load_scales("ds_table", d_scales, G)
+        offs_t = load_list("offs_t", offs)
+        xs_table = load_scales("xs_table", x_scales, T)
+        n1_t = load_list("n1_t", n1)
+        n2_t = load_list("n2_t", n2)
+        n3_t = load_list("n3_t", n3)
+        dw_table = load_words("dw_table", d_words, G)
+        xw_table = load_words("xw_table", x_words, T)
+        cand_t = load_list("cand_t", cand)
+        n4_t = load_list("n4_t", n4)
+        n5_t = load_list("n5_t", n5)
+        gs_t = sb.tile([P, PACK], F32, name="gs_t")
+        nc.gpsimd.dma_start(gs_t[:], gs.rearrange("(p t) o -> p (t o)", t=PACK))
+
+        h_win = [sb.tile([P, 2 * S], F32, name="h_win%d" % t) for t in range(PACK)]
+        for t in range(PACK):
+            nc.gpsimd.memset(h_win[t][:, S:], 0.0)
+
+        dk_bytes = gather_packed("dk_bytes", ds_table, k1_t, H, U8)
+        xq_bytes = gather_packed("xq_bytes", xs_table, offs_t, S, U8)
+        planes = sb.tile([P, H + S], U8, name="planes", align_bytes=64)
+        nc.vector.tensor_copy(
+            planes[:, :H].rearrange("p (t m) -> p t m", t=PACK), dk_bytes[:].rearrange("p (m t) -> p t m", t=PACK)
+        )
+        nc.vector.tensor_copy(planes[:, H:].bitcast(I32), xq_bytes[:].bitcast(I32))
+        place_odd_rows(planes, planes)
+        dk_picked = gather_packed("dk_picked", dw_table, k1_t, H, U32)
+        dk_words = sb.tile([P, H], U32, name="dk_words", align_bytes=64)
+        nc.vector.tensor_copy(
+            dk_words[:].rearrange("p (t c i) -> p c t i", t=PACK, i=4),
+            dk_picked[:].rearrange("p (c i t) -> p c t i", t=PACK, i=4),
+        )
+        xq_words = gather_packed("xq_words", xw_table, offs_t, S, U32)
+
+        h_ps = []
+        for t in range(PACK):
+            acc = ps.tile([P, S], F32, name="h_ps%d" % t, tag="bank%d" % t)
+            cols = slice(P * t, P * (t + 1))
+            nc.tensor.matmul_mx(
+                out=acc[:], lhsT=dk_words[:, cols].bitcast(FP8X4), lhsT_scale=planes[:, cols],
+                rhs=xq_words[:].bitcast(FP8X4), rhs_scale=planes[:, H:], start=True, stop=True,
+            )
+            h_ps.append(acc)
+
+        xc_words = gather_packed("xc_words", xw_table, cand_t, C, U32)
+
+        nc.scalar.activation(h_win[0][:, :S], h_ps[0][:], COPY, scale=SIXTEENTH)
+
+        st_win = [sb.tile([P, 2 * S], F32, name="st_win%d" % t) for t in range(PACK)]
+        z_bf = sb.tile([P, PACK * S], BF16, name="z_bf", align_bytes=64)
+
+        def leave_psum(t):
+            nc.vector.tensor_scalar(h_win[t][:, :S], h_ps[t][:], SIXTEENTH, None, ALU.mult)
+
+        def difference(t):
+            second = sb.tile([P, S], F32, name="second%d" % t)
+            nc.scalar.activation(st_win[t][:, S:], h_win[t][:].indirect(n1_t[:]), COPY)
+            nc.scalar.activation(second[:], h_win[t][:].indirect(n2_t[:]), COPY)
+            nc.vector.tensor_tensor(st_win[t][:, :S], st_win[t][:, S:], second[:], ALU.subtract)
+
+        def larger(t, lo, hi):
+            other = sb.tile([P, hi - lo], F32, name="other%d_%d" % (t, lo))
+            top = sb.tile([P, hi - lo], F32, name="top%d_%d" % (t, lo))
+            nc.scalar.activation(other[:], st_win[t][:].indirect(n3_t[:, lo // 16 : hi // 16]), COPY)
+            nc.vector.tensor_tensor(top[:], st_win[t][:, lo:hi], other[:], ALU.max)
+            nc.vector.tensor_scalar(z_bf[:, PACK * lo + t : PACK * hi : PACK], top[:], gs_t[:, t : t + 1], None, ALU.mult)
+
+        z_words = sb.tile([P, S], U32, name="z_words", align_bytes=64)
+        z_plane = sb.tile([P, S], U8, name="z_plane", align_bytes=64)
+
+        def quantise(lo, hi):
+            nc.vector.quantize_mx(out=z_words[:, lo:hi].bitcast(FP8X4), scales=z_plane[:, lo:hi], in_=z_bf[:, PACK * lo : PACK * hi])
+
+        leave_psum(1)
+        difference(0)
+        xc_bytes = gather_packed("xc_bytes", xs_table, cand_t, C, U8)
+        xc_plane = sb.tile([P, C], U8, name="xc_plane", align_bytes=64)
+        nc.vector.tensor_copy(xc_plane[:].bitcast(I32), xc_bytes[:].bitcast(I32))
+        place_odd_rows(xc_plane, xc_bytes)
+        leave_psum(2)
+        difference(1)
+        larger(0, 0, S)
+        leave_psum(3)
+        difference(2)
+        larger(1, 0, S)
+        difference(3)
+        larger(2, 0, S)
+        larger(3, 0, HALF)
+        larger(3, HALF, S)
+        quantise(0, HALF)
+        quantise(HALF, S)
+
+        s_win = [sb.tile([P, S], F32, name="s_win%d" % c) for c in range(C // P)]
+
+        def score(c, lo, hi, tag):
+            acc = ps.tile([P, hi - lo], F32, name="s_ps%d_%d" % (c, lo), tag=tag)
+            cols = slice(P * c, P * (c + 1))
+            nc.tensor.matmul_mx(
+                out=acc[:], lhsT=xc_words[:, cols].bitcast(FP8X4), lhsT_scale=xc_plane[:, cols],
+                rhs=z_words[:, lo:hi].bitcast(FP8X4), rhs_scale=z_plane[:, lo:hi], start=True, stop=True,
+            )
+            return acc
+
+        for lo in (0, HALF):
+            acc = score(0, lo, lo + HALF, "half%d" % lo)
+            nc.scalar.activation(s_win[0][:, lo : lo + HALF], acc[:], COPY, scale=SIXTEENTH)
+        for c in range(1, C // P):
+            acc = score(c, 0, S, "bank%d" % c)
+            nc.vector.tensor_scalar(s_win[c][:], acc[:], SIXTEENTH, None, ALU.mult)
+
+        ra = [sb.tile([P, W], F32, name="ra%d" % c) for c in range(C // P)]
+
+        def fetch(c):
+            old = sb.tile([P, W], F32, name="old%d" % c)
+            pa = sb.tile([P, W], F32, name="pa%d" % c)
+            nc.scalar.activation(old[:], s_win[c][:].indirect(n4_t[:]), COPY)
+            nc.scalar.activation(pa[:], s_win[c][:].indirect(n5_t[:]), COPY)
+            nc.vector.scalar_tensor_tensor(ra[c][:], pa[:], -0.5, old[:], ALU.mult, ALU.add)
+
+        def put(c):
+            nc.scalar.activation(s_win[c][:].indirect(n4_t[:]), ra[c][:], COPY)
+            nc.sync.dma_start(out[P * c : P * (c + 1), :], s_win[c][:])
+
+        fetch(0)
+        for c in range(1, C // P):
+            fetch(c)
+            put(c - 1)
+        put(C // P - 1)

@@ -26,6 +26,7 @@ def tile_picked_pqhcgapmxkdif_none_p_kernel(tc, x_words, x_scales, d_words, d_sc
     with ExitStack() as ctx:
         lists = ctx.enter_context(tc.tile_pool(name="lists", bufs=1))
         sb = ctx.enter_context(tc.tile_pool(name="sb", bufs=1))
+        turn = ctx.enter_context(tc.tile_pool(name="turn", bufs=1))
         ps = ctx.enter_context(tc.psum_pool(name="ps", bufs=1))
 
         def load_list(name, src):
@@ -36,7 +37,7 @@ def tile_picked_pqhcgapmxkdif_none_p_kernel(tc, x_words, x_scales, d_words, d_sc
         def load_scales(name, src, width):
             t = sb.tile([P, width], U8, name=name, align_bytes=64)
             rows = src[0].bitcast(I32)
-            nc.sync.dma_start(t[:].bitcast(I32), rows.unsqueeze(1).broadcast_to([16, 8, width // 4]))
+            nc.scalar.dma_start(t[:].bitcast(I32), rows.unsqueeze(1).broadcast_to([16, 8, width // 4]))
             return t
 
         def load_words(name, src, width):
@@ -44,25 +45,26 @@ def tile_picked_pqhcgapmxkdif_none_p_kernel(tc, x_words, x_scales, d_words, d_sc
             nc.sync.dma_start(t[:].bitcast(I32), src[0].rearrange("p n r -> p (n r)").bitcast(I32))
             return t
 
-        def gather_packed(name, table, offsets, count, dtype):
-            t = sb.tile([P, count], dtype, name=name, align_bytes=64)
+        def gather_packed(t, table, offsets):
             nc.vector.tensor_copy(t[:], table[:].indirect(offsets[:]))
-            return t
 
-        def place_odd_rows(dst, src):
-            for row in (1, 2, 3):
-                nc.scalar.dma_start(dst[row:P:32, :].bitcast(I32), src[8 * row : P : 32, :].bitcast(I32))
+        def place_rows(queue, dst, src, moves):
+            for row, found in moves:
+                queue.dma_start(dst[row:P:32, :].bitcast(I32), src[found:P:32, :].bitcast(I32))
 
         k1_t = load_list("k1_t", k1)
         ds_table = load_scales("ds_table", d_scales, G)
         offs_t = load_list("offs_t", offs)
-        xs_table = load_scales("xs_table", x_scales, T)
-        n1_t = load_list("n1_t", n1)
-        n2_t = load_list("n2_t", n2)
-        n3_t = load_list("n3_t", n3)
+        xs_table = sb.tile([P, T], U8, name="xs_table", align_bytes=64)
+        for q in range(4):
+            rows = x_scales[0, 4 * q : 4 * q + 4, :].bitcast(I32)
+            (nc.sync if q < 2 else nc.scalar).dma_start(xs_table[32 * q : 32 * q + 32, :].bitcast(I32), rows.unsqueeze(0).broadcast_to([8, 4, T // 4]))
         dw_table = load_words("dw_table", d_words, G)
         xw_table = load_words("xw_table", x_words, T)
         cand_t = load_list("cand_t", cand)
+        n1_t = load_list("n1_t", n1)
+        n2_t = load_list("n2_t", n2)
+        n3_t = load_list("n3_t", n3)
         n4_t = load_list("n4_t", n4)
         n5_t = load_list("n5_t", n5)
         gs_t = sb.tile([P, PACK], F32, name="gs_t")
@@ -70,23 +72,31 @@ def tile_picked_pqhcgapmxkdif_none_p_kernel(tc, x_words, x_scales, d_words, d_sc
 
         h_win = [sb.tile([P, 2 * S], F32, name="h_win%d" % t) for t in range(PACK)]
         for t in range(PACK):
-            nc.gpsimd.memset(h_win[t][:, S:], 0.0)
+            nc.vector.memset(h_win[t][:, S:], 0.0)
 
-        dk_bytes = gather_packed("dk_bytes", ds_table, k1_t, H, U8)
-        xq_bytes = gather_packed("xq_bytes", xs_table, offs_t, S, U8)
-        planes = sb.tile([P, H + S], U8, name="planes", align_bytes=64)
+        dk_bytes = sb.tile([P, H], U8, align_bytes=64)
+        gather_packed(dk_bytes, ds_table, k1_t)
+        planes = sb.tile([P, H], U8, name="planes", align_bytes=64)
         nc.vector.tensor_copy(
             planes[:, :H].rearrange("p (t m) -> p t m", t=PACK), dk_bytes[:].rearrange("p (m t) -> p t m", t=PACK)
         )
-        nc.vector.tensor_copy(planes[:, H:].bitcast(I32), xq_bytes[:].bitcast(I32))
-        place_odd_rows(planes, planes)
-        dk_picked = gather_packed("dk_picked", dw_table, k1_t, H, U32)
+        place_rows(nc.scalar, planes, planes, ((1, 8), (2, 16), (3, 24)))
+        xq_plane = sb.tile([P, S], U8, align_bytes=64)
+        gather_packed(xq_plane, xs_table, offs_t)
+        dk_picked = turn.tile([P, H], U32, align_bytes=64, offset=0)
+        gather_packed(dk_picked, dw_table, k1_t)
         dk_words = sb.tile([P, H], U32, name="dk_words", align_bytes=64)
         nc.vector.tensor_copy(
             dk_words[:].rearrange("p (t c i) -> p c t i", t=PACK, i=4),
             dk_picked[:].rearrange("p (c i t) -> p c t i", t=PACK, i=4),
         )
-        xq_words = gather_packed("xq_words", xw_table, offs_t, S, U32)
+        xq_words = turn.tile([P, S], U32, align_bytes=64, offset=0)
+        gather_packed(xq_words, xw_table, offs_t)
+        xc_bytes = turn.tile([P, C], U8, align_bytes=64, offset=4 * S)
+        gather_packed(xc_bytes, xs_table, cand_t)
+        xc_plane = sb.tile([P, C], U8, name="xc_plane", align_bytes=64)
+        nc.vector.tensor_copy(xc_plane[:].bitcast(I32), xc_bytes[:].bitcast(I32))
+        place_rows(nc.sync, xc_plane, xc_bytes, ((2, 18), (3, 19)))
 
         h_ps = []
         for t in range(PACK):
@@ -94,11 +104,10 @@ def tile_picked_pqhcgapmxkdif_none_p_kernel(tc, x_words, x_scales, d_words, d_sc
             cols = slice(P * t, P * (t + 1))
             nc.tensor.matmul_mx(
                 out=acc[:], lhsT=dk_words[:, cols].bitcast(FP8X4), lhsT_scale=planes[:, cols],
-                rhs=xq_words[:].bitcast(FP8X4), rhs_scale=planes[:, H:], start=True, stop=True,
+                rhs=xq_words[:].bitcast(FP8X4), rhs_scale=xq_plane[:], start=True, stop=True,
             )
             h_ps.append(acc)
 
-        xc_words = gather_packed("xc_words", xw_table, cand_t, C, U32)
 
         nc.scalar.activation(h_win[0][:, :S], h_ps[0][:], COPY, scale=SIXTEENTH)
 
@@ -109,7 +118,7 @@ def tile_picked_pqhcgapmxkdif_none_p_kernel(tc, x_words, x_scales, d_words, d_sc
             nc.vector.tensor_scalar(h_win[t][:, :S], h_ps[t][:], SIXTEENTH, None, ALU.mult)
 
         def difference(t):
-            second = sb.tile([P, S], F32, name="second%d" % t)
+            second = sb.tile([P, S], F32, name="second%d" % t, tag="second%d" % t, align_bytes=64)
             nc.scalar.activation(st_win[t][:, S:], h_win[t][:].indirect(n1_t[:]), COPY)
             nc.scalar.activation(second[:], h_win[t][:].indirect(n2_t[:]), COPY)
             nc.vector.tensor_tensor(st_win[t][:, :S], st_win[t][:, S:], second[:], ALU.subtract)
@@ -129,18 +138,17 @@ def tile_picked_pqhcgapmxkdif_none_p_kernel(tc, x_words, x_scales, d_words, d_sc
 
         leave_psum(1)
         difference(0)
-        xc_bytes = gather_packed("xc_bytes", xs_table, cand_t, C, U8)
-        xc_plane = sb.tile([P, C], U8, name="xc_plane", align_bytes=64)
-        nc.vector.tensor_copy(xc_plane[:].bitcast(I32), xc_bytes[:].bitcast(I32))
-        place_odd_rows(xc_plane, xc_bytes)
         leave_psum(2)
+        leave_psum(3)
+        xc_words = sb.tile([P, C], U32, tag="second0", align_bytes=64)
+        gather_packed(xc_words, xw_table, cand_t)
         difference(1)
         larger(0, 0, S)
-        leave_psum(3)
         difference(2)
         larger(1, 0, S)
         difference(3)
-        larger(2, 0, S)
+        larger(2, 0, HALF)
+        larger(2, HALF, S)
         larger(3, 0, HALF)
         larger(3, HALF, S)
         quantise(0, HALF)

@@ -18,7 +18,9 @@ COPY = mybir.ActivationFunctionType.Copy
 P = 128
 PACK = 4
 HALF = S // 2
+PIECES = ((0, 128), (128, 192), (192, 256))
 SIXTEENTH = 0.0625
+MOVES = ((1, 8), (2, 16), (3, 24))
 
 
 def tile_picked_pqhcgapmxkdif_none_p_kernel(tc, x_words, x_scales, d_words, d_scales, gs, offs, k1, n1, n2, n3, cand, n4, n5, out):
@@ -26,7 +28,6 @@ def tile_picked_pqhcgapmxkdif_none_p_kernel(tc, x_words, x_scales, d_words, d_sc
     with ExitStack() as ctx:
         lists = ctx.enter_context(tc.tile_pool(name="lists", bufs=1))
         sb = ctx.enter_context(tc.tile_pool(name="sb", bufs=1))
-        turn = ctx.enter_context(tc.tile_pool(name="turn", bufs=1))
         ps = ctx.enter_context(tc.psum_pool(name="ps", bufs=1))
 
         def load_list(name, src):
@@ -41,7 +42,7 @@ def tile_picked_pqhcgapmxkdif_none_p_kernel(tc, x_words, x_scales, d_words, d_sc
             return t
 
         def load_words(name, src, width):
-            t = sb.tile([P, width], U32, name=name, align_bytes=64)
+            t = sb.tile([P, width], U32, name=name, tag=name, align_bytes=64)
             nc.sync.dma_start(t[:].bitcast(I32), src[0].rearrange("p n r -> p (n r)").bitcast(I32))
             return t
 
@@ -52,18 +53,15 @@ def tile_picked_pqhcgapmxkdif_none_p_kernel(tc, x_words, x_scales, d_words, d_sc
             for row, found in moves:
                 queue.dma_start(dst[row:P:32, :].bitcast(I32), src[found:P:32, :].bitcast(I32))
 
+        offs_t = load_list("offs_t", offs)
+        xs_table = load_scales("xs_table", x_scales, T)
         k1_t = load_list("k1_t", k1)
         ds_table = load_scales("ds_table", d_scales, G)
-        offs_t = load_list("offs_t", offs)
-        xs_table = sb.tile([P, T], U8, name="xs_table", align_bytes=64)
-        for q in range(4):
-            rows = x_scales[0, 4 * q : 4 * q + 4, :].bitcast(I32)
-            (nc.sync if q < 2 else nc.scalar).dma_start(xs_table[32 * q : 32 * q + 32, :].bitcast(I32), rows.unsqueeze(0).broadcast_to([8, 4, T // 4]))
-        dw_table = load_words("dw_table", d_words, G)
-        xw_table = load_words("xw_table", x_words, T)
         cand_t = load_list("cand_t", cand)
         n1_t = load_list("n1_t", n1)
         n2_t = load_list("n2_t", n2)
+        dw_table = load_words("dw_table", d_words, G)
+        xw_table = load_words("xw_table", x_words, T)
         n3_t = load_list("n3_t", n3)
         n4_t = load_list("n4_t", n4)
         n5_t = load_list("n5_t", n5)
@@ -71,47 +69,52 @@ def tile_picked_pqhcgapmxkdif_none_p_kernel(tc, x_words, x_scales, d_words, d_sc
         nc.gpsimd.dma_start(gs_t[:], gs.rearrange("(p t) o -> p (t o)", t=PACK))
 
         h_win = [sb.tile([P, 2 * S], F32, name="h_win%d" % t) for t in range(PACK)]
-        for t in range(PACK):
+        for t in range(PACK - 1):
             nc.vector.memset(h_win[t][:, S:], 0.0)
+        nc.scalar.activation(h_win[PACK - 1][:, S:], h_win[0][:, S:], COPY)
 
-        dk_bytes = sb.tile([P, H], U8, align_bytes=64)
+        planes = sb.tile([P, H + S], U8, name="planes", align_bytes=64)
+        xq_bytes = sb.tile([P, S], U8, align_bytes=64)
+        gather_packed(xq_bytes, xs_table, offs_t)
+        nc.vector.tensor_copy(planes[:, H:].bitcast(I32), xq_bytes[:].bitcast(I32))
+        dk_bytes = sb.tile([P, H], U8, tag="dk_picked", align_bytes=64)
         gather_packed(dk_bytes, ds_table, k1_t)
-        planes = sb.tile([P, H], U8, name="planes", align_bytes=64)
         nc.vector.tensor_copy(
             planes[:, :H].rearrange("p (t m) -> p t m", t=PACK), dk_bytes[:].rearrange("p (m t) -> p t m", t=PACK)
         )
-        place_rows(nc.scalar, planes, planes, ((1, 8), (2, 16), (3, 24)))
-        xq_plane = sb.tile([P, S], U8, align_bytes=64)
-        gather_packed(xq_plane, xs_table, offs_t)
-        dk_picked = turn.tile([P, H], U32, align_bytes=64, offset=0)
+        place_rows(nc.scalar, planes, planes, MOVES)
+        dk_picked = sb.tile([P, H], U32, tag="dk_picked", align_bytes=64)
         gather_packed(dk_picked, dw_table, k1_t)
+        dk_first = sb.tile([P, P], U32, tag="dk_first", align_bytes=64)
         dk_words = sb.tile([P, H], U32, name="dk_words", align_bytes=64)
-        nc.vector.tensor_copy(
-            dk_words[:].rearrange("p (t c i) -> p c t i", t=PACK, i=4),
-            dk_picked[:].rearrange("p (c i t) -> p c t i", t=PACK, i=4),
-        )
-        xq_words = turn.tile([P, S], U32, align_bytes=64, offset=0)
+        xq_words = sb.tile([P, S], U32, tag="dw_table", align_bytes=64)
         gather_packed(xq_words, xw_table, offs_t)
-        xc_bytes = turn.tile([P, C], U8, align_bytes=64, offset=4 * S)
-        gather_packed(xc_bytes, xs_table, cand_t)
-        xc_plane = sb.tile([P, C], U8, name="xc_plane", align_bytes=64)
-        nc.vector.tensor_copy(xc_plane[:].bitcast(I32), xc_bytes[:].bitcast(I32))
-        place_rows(nc.sync, xc_plane, xc_bytes, ((2, 18), (3, 19)))
-
+        nc.vector.tensor_copy(dk_first[:], dk_picked[:, 0:H:PACK])
+        nc.vector.tensor_copy(
+            dk_words[:].rearrange("p (t c i) -> p c t i", t=PACK, i=4)[:, :, 1:, :],
+            dk_picked[:].rearrange("p (c i t) -> p c t i", t=PACK, i=4)[:, :, 1:, :],
+        )
         h_ps = []
         for t in range(PACK):
             acc = ps.tile([P, S], F32, name="h_ps%d" % t, tag="bank%d" % t)
             cols = slice(P * t, P * (t + 1))
             nc.tensor.matmul_mx(
-                out=acc[:], lhsT=dk_words[:, cols].bitcast(FP8X4), lhsT_scale=planes[:, cols],
-                rhs=xq_words[:].bitcast(FP8X4), rhs_scale=xq_plane[:], start=True, stop=True,
+                out=acc[:], lhsT=(dk_words[:, cols] if t else dk_first[:]).bitcast(FP8X4), lhsT_scale=planes[:, cols],
+                rhs=xq_words[:].bitcast(FP8X4), rhs_scale=planes[:, H:], start=True, stop=True,
             )
             h_ps.append(acc)
 
+        xc_bytes = sb.tile([P, C], U8, tag="dk_first", align_bytes=64)
+        gather_packed(xc_bytes, xs_table, cand_t)
+        xc_plane = sb.tile([P, C], U8, name="xc_plane", align_bytes=64)
+        nc.vector.tensor_copy(xc_plane[:].bitcast(I32), xc_bytes[:].bitcast(I32))
+        place_rows(nc.sync, xc_plane, xc_bytes, MOVES)
 
         nc.scalar.activation(h_win[0][:, :S], h_ps[0][:], COPY, scale=SIXTEENTH)
 
-        st_win = [sb.tile([P, 2 * S], F32, name="st_win%d" % t) for t in range(PACK)]
+        st_win = [sb.tile([P, 2 * S if t < PACK - 1 else S], F32, name="st_win%d" % t) for t in range(PACK)]
+        last_first = sb.tile([P, S], F32)
+        first = [st_win[t][:, S:] for t in range(PACK - 1)] + [last_first[:]]
         z_bf = sb.tile([P, PACK * S], BF16, name="z_bf", align_bytes=64)
 
         def leave_psum(t):
@@ -119,9 +122,9 @@ def tile_picked_pqhcgapmxkdif_none_p_kernel(tc, x_words, x_scales, d_words, d_sc
 
         def difference(t):
             second = sb.tile([P, S], F32, name="second%d" % t, tag="second%d" % t, align_bytes=64)
-            nc.scalar.activation(st_win[t][:, S:], h_win[t][:].indirect(n1_t[:]), COPY)
+            nc.scalar.activation(first[t], h_win[t][:].indirect(n1_t[:]), COPY)
             nc.scalar.activation(second[:], h_win[t][:].indirect(n2_t[:]), COPY)
-            nc.vector.tensor_tensor(st_win[t][:, :S], st_win[t][:, S:], second[:], ALU.subtract)
+            nc.vector.tensor_tensor(st_win[t][:, :S], first[t], second[:], ALU.subtract)
 
         def larger(t, lo, hi):
             other = sb.tile([P, hi - lo], F32, name="other%d_%d" % (t, lo))
@@ -149,10 +152,10 @@ def tile_picked_pqhcgapmxkdif_none_p_kernel(tc, x_words, x_scales, d_words, d_sc
         difference(3)
         larger(2, 0, HALF)
         larger(2, HALF, S)
-        larger(3, 0, HALF)
-        larger(3, HALF, S)
-        quantise(0, HALF)
-        quantise(HALF, S)
+        for lo, hi in PIECES:
+            larger(3, lo, hi)
+        for lo, hi in PIECES:
+            quantise(lo, hi)
 
         s_win = [sb.tile([P, S], F32, name="s_win%d" % c) for c in range(C // P)]
 
@@ -165,9 +168,9 @@ def tile_picked_pqhcgapmxkdif_none_p_kernel(tc, x_words, x_scales, d_words, d_sc
             )
             return acc
 
-        for lo in (0, HALF):
-            acc = score(0, lo, lo + HALF, "half%d" % lo)
-            nc.scalar.activation(s_win[0][:, lo : lo + HALF], acc[:], COPY, scale=SIXTEENTH)
+        for lo, hi in PIECES:
+            acc = score(0, lo, hi, "piece%d" % lo)
+            nc.scalar.activation(s_win[0][:, lo:hi], acc[:], COPY, scale=SIXTEENTH)
         for c in range(1, C // P):
             acc = score(c, 0, S, "bank%d" % c)
             nc.vector.tensor_scalar(s_win[c][:], acc[:], SIXTEENTH, None, ALU.mult)

from contextlib import ExitStack

import concourse.mybir as mybir

K, T, S, G, H, C, W = 512, 1024, 256, 2048, 512, 512, 192
FLOPS = 2 * K * H * S + 2 * K * C * S

F32 = mybir.dt.float32
BF16 = mybir.dt.bfloat16
I32 = mybir.dt.int32
U32 = mybir.dt.uint32
U16 = mybir.dt.uint16
U8 = mybir.dt.uint8
FP8X4 = mybir.dt.float8_e4m3fn_x4
ALU = mybir.AluOpType
COPY = mybir.ActivationFunctionType.Copy

P = 128
PACK = 4
HALF = S // 2
PIECES = ((0, 128), (128, 192), (192, 256))
SIXTEENTH = 0.0625
MOVES = ((1, 8), (2, 16), (3, 24))


def tile_picked_pqhcgapmxkdif_none_p_kernel(tc, x_words, x_scales, d_words, d_scales, gs, offs, k1, n1, n2, n3, cand, n4, n5, out):
    nc = tc.nc
    with ExitStack() as ctx:
        lists = ctx.enter_context(tc.tile_pool(name="lists", bufs=1))
        sb = ctx.enter_context(tc.tile_pool(name="sb", bufs=1))
        ps = ctx.enter_context(tc.psum_pool(name="ps", bufs=1))

        def load_list(name, src):
            t = lists.tile(list(src.shape), U16, name=name)
            nc.sync.dma_start(t[:], src)
            return t

        def load_scales(name, src, width):
            t = sb.tile([P, width], U8, name=name, align_bytes=64)
            rows = src[0].bitcast(I32)
            nc.scalar.dma_start(t[:].bitcast(I32), rows.unsqueeze(1).broadcast_to([16, 8, width // 4]))
            return t

        def load_words(name, src, width):
            t = sb.tile([P, width], U32, name=name, tag=name, align_bytes=64)
            nc.sync.dma_start(t[:].bitcast(I32), src[0].rearrange("p n r -> p (n r)").bitcast(I32))
            return t

        def gather_packed(t, table, offsets):
            nc.vector.tensor_copy(t[:], table[:].indirect(offsets[:]))

        def place_rows(queue, dst, src, moves):
            for row, found in moves:
                queue.dma_start(dst[row:P:32, :].bitcast(I32), src[found:P:32, :].bitcast(I32))

        offs_t = load_list("offs_t", offs)
        xs_table = load_scales("xs_table", x_scales, T)
        k1_t = load_list("k1_t", k1)
        ds_table = load_scales("ds_table", d_scales, G)
        cand_t = load_list("cand_t", cand)
        n1_t = load_list("n1_t", n1)
        n2_t = load_list("n2_t", n2)
        dw_table = load_words("dw_table", d_words, G)
        xw_table = load_words("xw_table", x_words, T)
        n3_t = load_list("n3_t", n3)
        n4_t = load_list("n4_t", n4)
        n5_t = load_list("n5_t", n5)
        gs_t = sb.tile([P, PACK], F32, name="gs_t")
        nc.gpsimd.dma_start(gs_t[:], gs.rearrange("(p t) o -> p (t o)", t=PACK))

        h_win = [sb.tile([P, 2 * S], F32, name="h_win%d" % t) for t in range(PACK)]
        for t in range(PACK - 1):
            nc.vector.memset(h_win[t][:, S:], 0.0)
        nc.scalar.activation(h_win[PACK - 1][:, S:], h_win[0][:, S:], COPY)

        planes = sb.tile([P, H + S], U8, name="planes", align_bytes=64)
        xq_bytes = sb.tile([P, S], U8, align_bytes=64)
        gather_packed(xq_bytes, xs_table, offs_t)
        nc.vector.tensor_copy(planes[:, H:].bitcast(I32), xq_bytes[:].bitcast(I32))
        dk_bytes = sb.tile([P, H], U8, tag="dk_picked", align_bytes=64)
        gather_packed(dk_bytes, ds_table, k1_t)
        nc.vector.tensor_copy(
            planes[:, :H].rearrange("p (t m) -> p t m", t=PACK), dk_bytes[:].rearrange("p (m t) -> p t m", t=PACK)
        )
        place_rows(nc.scalar, planes, planes, MOVES)
        dk_picked = sb.tile([P, H], U32, tag="dk_picked", align_bytes=64)
        gather_packed(dk_picked, dw_table, k1_t)
        dk_first = sb.tile([P, P], U32, tag="dk_first", align_bytes=64)
        dk_words = sb.tile([P, H], U32, name="dk_words", align_bytes=64)
        xq_words = sb.tile([P, S], U32, tag="dw_table", align_bytes=64)
        gather_packed(xq_words, xw_table, offs_t)
        nc.vector.tensor_copy(dk_first[:], dk_picked[:, 0:H:PACK])
        nc.vector.tensor_copy(
            dk_words[:].rearrange("p (t c i) -> p c t i", t=PACK, i=4)[:, :, 1:, :],
            dk_picked[:].rearrange("p (c i t) -> p c t i", t=PACK, i=4)[:, :, 1:, :],
        )
        h_ps = []
        for t in range(PACK):
            acc = ps.tile([P, S], F32, name="h_ps%d" % t, tag="bank%d" % t)
            cols = slice(P * t, P * (t + 1))
            nc.tensor.matmul_mx(
                out=acc[:], lhsT=(dk_words[:, cols] if t else dk_first[:]).bitcast(FP8X4), lhsT_scale=planes[:, cols],
                rhs=xq_words[:].bitcast(FP8X4), rhs_scale=planes[:, H:], start=True, stop=True,
            )
            h_ps.append(acc)

        xc_bytes = sb.tile([P, C], U8, tag="dk_first", align_bytes=64)
        gather_packed(xc_bytes, xs_table, cand_t)
        xc_plane = sb.tile([P, C], U8, name="xc_plane", align_bytes=64)
        nc.vector.tensor_copy(xc_plane[:].bitcast(I32), xc_bytes[:].bitcast(I32))
        place_rows(nc.sync, xc_plane, xc_bytes, MOVES)

        nc.scalar.activation(h_win[0][:, :S], h_ps[0][:], COPY, scale=SIXTEENTH)

        st_win = [sb.tile([P, 2 * S if t < PACK - 1 else S], F32, name="st_win%d" % t) for t in range(PACK)]
        last_first = sb.tile([P, S], F32)
        first = [st_win[t][:, S:] for t in range(PACK - 1)] + [last_first[:]]
        z_bf = sb.tile([P, PACK * S], BF16, name="z_bf", align_bytes=64)

        def leave_psum(t):
            nc.vector.tensor_scalar(h_win[t][:, :S], h_ps[t][:], SIXTEENTH, None, ALU.mult)

        def difference(t):
            second = sb.tile([P, S], F32, name="second%d" % t, tag="second%d" % t, align_bytes=64)
            nc.scalar.activation(first[t], h_win[t][:].indirect(n1_t[:]), COPY)
            nc.scalar.activation(second[:], h_win[t][:].indirect(n2_t[:]), COPY)
            nc.vector.tensor_tensor(st_win[t][:, :S], first[t], second[:], ALU.subtract)

        def larger(t, lo, hi):
            other = sb.tile([P, hi - lo], F32, name="other%d_%d" % (t, lo))
            top = sb.tile([P, hi - lo], F32, name="top%d_%d" % (t, lo))
            nc.scalar.activation(other[:], st_win[t][:].indirect(n3_t[:, lo // 16 : hi // 16]), COPY)
            nc.vector.tensor_tensor(top[:], st_win[t][:, lo:hi], other[:], ALU.max)
            nc.vector.tensor_scalar(z_bf[:, PACK * lo + t : PACK * hi : PACK], top[:], gs_t[:, t : t + 1], None, ALU.mult)

        z_words = sb.tile([P, S], U32, name="z_words", align_bytes=64)
        z_plane = sb.tile([P, S], U8, name="z_plane", align_bytes=64)

        def quantise(lo, hi):
            nc.vector.quantize_mx(out=z_words[:, lo:hi].bitcast(FP8X4), scales=z_plane[:, lo:hi], in_=z_bf[:, PACK * lo : PACK * hi])

        leave_psum(1)
        difference(0)
        leave_psum(2)
        leave_psum(3)
        xc_words = sb.tile([P, C], U32, tag="second0", align_bytes=64)
        gather_packed(xc_words, xw_table, cand_t)
        difference(1)
        larger(0, 0, S)
        difference(2)
        larger(1, 0, S)
        difference(3)
        larger(2, 0, HALF)
        larger(2, HALF, S)
        for lo, hi in PIECES:
            larger(3, lo, hi)
        for lo, hi in PIECES:
            quantise(lo, hi)

        s_win = [sb.tile([P, S], F32, name="s_win%d" % c) for c in range(C // P)]

        def score(c, lo, hi, tag):
            acc = ps.tile([P, hi - lo], F32, name="s_ps%d_%d" % (c, lo), tag=tag)
            cols = slice(P * c, P * (c + 1))
            nc.tensor.matmul_mx(
                out=acc[:], lhsT=xc_words[:, cols].bitcast(FP8X4), lhsT_scale=xc_plane[:, cols],
                rhs=z_words[:, lo:hi].bitcast(FP8X4), rhs_scale=z_plane[:, lo:hi], start=True, stop=True,
            )
            return acc

        for lo, hi in PIECES:
            acc = score(0, lo, hi, "piece%d" % lo)
            nc.scalar.activation(s_win[0][:, lo:hi], acc[:], COPY, scale=SIXTEENTH)
        for c in range(1, C // P):
            acc = score(c, 0, S, "bank%d" % c)
            nc.vector.tensor_scalar(s_win[c][:], acc[:], SIXTEENTH, None, ALU.mult)

        ra = [sb.tile([P, W], F32, name="ra%d" % c) for c in range(C // P)]

        def fetch(c):
            old = sb.tile([P, W], F32, name="old%d" % c)
            pa = sb.tile([P, W], F32, name="pa%d" % c)
            nc.scalar.activation(old[:], s_win[c][:].indirect(n4_t[:]), COPY)
            nc.scalar.activation(pa[:], s_win[c][:].indirect(n5_t[:]), COPY)
            nc.vector.scalar_tensor_tensor(ra[c][:], pa[:], -0.5, old[:], ALU.mult, ALU.add)

        def put(c):
            nc.scalar.activation(s_win[c][:].indirect(n4_t[:]), ra[c][:], COPY)
            nc.sync.dma_start(out[P * c : P * (c + 1), :], s_win[c][:])

        fetch(0)
        for c in range(1, C // P):
            fetch(c)
            put(c - 1)
        put(C // P - 1)
